import numpy as np, ml_dtypes
CORES = [6,14,30,38,62,70,86,94,102]
N = 9
F = 128
def setup_inputs(rng):
    return {"ah": rng.standard_normal((N, 128, 128), dtype=np.float32).astype(ml_dtypes.bfloat16), "al": (rng.standard_normal((N, 128, 128), dtype=np.float32) / 256).astype(ml_dtypes.bfloat16), "bh": rng.standard_normal((N, 128, F), dtype=np.float32).astype(ml_dtypes.bfloat16), "bl": (rng.standard_normal((N, 128, F), dtype=np.float32) / 256).astype(ml_dtypes.bfloat16)}
def setup_inputs_big(rng):
    d = setup_inputs(rng)
    for k in ("ah", "al", "bh", "bl"): d[k] = (d[k].astype(np.float32) * 1024.0).astype(d[k].dtype)
    return d
def setup_inputs_small(rng):
    d = setup_inputs(rng)
    for k in ("ah", "al", "bh", "bl"): d[k] = (d[k].astype(np.float32) * (1 / 1024.0)).astype(d[k].dtype)
    return d
def setup_inputs_apart(rng):
    d = setup_inputs(rng)
    f = (10.0 ** rng.permutation(np.linspace(-1.5, 1.5, N))).astype(np.float32).reshape(N, 1, 1)
    for k in ("ah", "al", "bh", "bl"): d[k] = (d[k].astype(np.float32) * f).astype(d[k].dtype)
    return d
def reference(ah, al, bh, bl):
    AH, AL, BH, BL = ah.astype(np.float64), al.astype(np.float64), bh.astype(np.float64), bl.astype(np.float64)
    s = sum((AH[j] + AL[j]).T @ (BH[j] + BL[j]) for j in range(N))
    s = s.astype(np.float32 if ah.dtype != np.float64 else np.float64)
    return {"y": np.broadcast_to(s, (N,) + s.shape)}

@@ -1,0 +1,146 @@
+from concourse.bass import DstId, RemoteDMATransfer
+from concourse.mybir import AluOpType
+
+P = 128
+NS = 8
+RW = P // NS
+
+SCRATCH = {
+    "sah": ("sbuf", [P, P], "bfloat16"),
+    "sal": ("sbuf", [P, P], "bfloat16"),
+    "sbh": ("sbuf", [P, P], "bfloat16"),
+    "sbl": ("sbuf", [P, P], "bfloat16"),
+    "acc": ("psum", [P, 512], "float32"),
+    "own": ("psum", [P, 512], "float32"),
+    "part": ("sbuf", [P, P], "float32"),
+    "stage": ("dram", [NS, P, RW], "float32"),
+    "land": ("dram", [NS, P, RW], "float32"),
+    "res": ("dram", [NS, P, RW], "float32"),
+    "seed": ("sbuf", [P, P + 1], "float32"),
+    "diag": ("dram", [P + 1, P], "float32"),
+    "eye": ("sbuf", [P, P], "float32"),
+    "h1": ("sbuf", [P, 64], "float32"),
+    "h2": ("sbuf", [P, 32], "float32"),
+    "sel": ("sbuf", [P, RW], "float32"),
+    "gath": ("sbuf", [P, P], "float32"),
+    "mine": ("sbuf", [P, P], "float32"),
+    "tot": ("sbuf", [P, P], "float32"),
+}
+SEMAPHORES = ["ldh", "ldl", "mm", "cp", "staged", "arr", "got", "loc", "st", "st2",
+              "zs", "w1", "w2", "vs", "sk", "gs", "om", "ms", "ts"]
+
+
+def _bits(m):
+    return [b for b in range(m.bit_length()) if (m >> b) & 1]
+
+
+def rank_program(g, core, T, topo):
+    rank = T.rank_of(core)
+    if rank is None:
+        return
+    S = T.sem
+    cores = list(T.cores)
+    n = len(cores)
+    others = [r for r in range(n) if r != rank]
+    for r in others:
+        if not topo.may_write(core, cores[r]):
+            raise ValueError("this plan needs every rank core to reach every other one by a write of its own")
+
+    peers = [sum(1 for b in cores if topo.same_plane(topo.chip(a), topo.chip(b))) for a in cores]
+    idle = max(r for r in range(n) if peers[r] == max(peers))
+    owners = [r for r in range(n) if r != idle]
+    my = owners.index(rank) if rank != idle else None
+
+    def dst_id(r):
+        rid, pid, _ = topo.addr(cores[r])
+        return DstId(rid=rid, pnc=pid)
+
+    wire = topo.mask(core, cores[others[0]])
+    for r in others:
+        wire &= topo.mask(core, cores[r])
+    eng = _bits(wire)
+    ne = len(eng)
+
+    g.sync.dma_start(T.sah[:, :], T.ah[:, :]).then_inc(S.ldh, 16)
+    g.scalar.dma_start(T.sbh[:, :], T.bh[:, :]).then_inc(S.ldh, 16)
+    g.sync.dma_start(T.sal[:, :], T.al[:, :]).then_inc(S.ldl, 16)
+    g.scalar.dma_start(T.sbl[:, :], T.bl[:, :]).then_inc(S.ldl, 16)
+
+    acc = T.acc[:, 0:P]
+    g.tensor.wait_ge(S.ldh, 32)
+    g.tensor.matmul(acc, T.sah[:, :], T.sbh[:, :], start=True, stop=False)
+    g.tensor.wait_ge(S.ldl, 32)
+    g.tensor.matmul(acc, T.sah[:, :], T.sbl[:, :], start=False, stop=False)
+    g.tensor.matmul(acc, T.sal[:, :], T.sbh[:, :], start=False, stop=False)
+    g.tensor.matmul(acc, T.sal[:, :], T.sbl[:, :], start=False, stop=True).then_inc(S.mm, 1)
+
+    if my is not None:
+        g.vector.memset(T.seed[:, 0:1], 1.0).then_inc(S.zs, 1)
+        g.vector.memset(T.seed[:, 1:P + 1], 0.0).then_inc(S.zs, 1)
+        g.scalar.wait_ge(S.zs, 2)
+        g.scalar.dma_start(T.diag[:, :], T.seed[:, :]).then_inc(S.w1, 16)
+
+    g.vector.wait_ge(S.mm, 1)
+    g.vector.tensor_copy(T.part[:, :], acc).then_inc(S.cp, 1)
+    g.sync.wait_ge(S.cp, 1)
+    g.sync.dma_start(T.stage[:, :, :], T.part[:, :]).then_inc(S.staged, 16)
+
+    g.wait_ge(S.staged, 16)
+    sends = []
+    for s, o in enumerate(owners):
+        if o == rank:
+            continue
+        slot = rank if rank < o else rank - 1
+        sends.append(RemoteDMATransfer(dst_ids=[dst_id(o)], dma_engine_mask=1 << eng[s % ne], remote_sem=S.arr,
+                                       src=T.stage[s], dst=T.land[slot]))
+    g.remote_dma_fused(sends, local_sem=S.loc)
+    left = len(sends)
+
+    if my is not None:
+        lo, hi = RW * my, RW * (my + 1)
+        g.scalar.wait_ge(S.w1, 16)
+        g.scalar.wait_ge(S.staged, 16)
+        g.scalar.dma_start(T.eye[:, :], T.diag[0:P, :]).then_inc(S.w2, 16)
+        g.scalar.wait_ge(S.cp, 1)
+        g.scalar.dma_start(T.mine[0:RW, :], T.part[lo:hi, :]).then_inc(S.ms, 16)
+        g.vector.wait_ge(S.w2, 16)
+        g.vector.tensor_tensor(T.h1[:, :], T.eye[:, 0:64], T.eye[:, 64:128], AluOpType.add).then_inc(S.vs, 1)
+        g.vector.wait_ge(S.vs, 1)
+        g.vector.tensor_tensor(T.h2[:, :], T.h1[:, 0:32], T.h1[:, 32:64], AluOpType.add).then_inc(S.vs, 1)
+        g.vector.wait_ge(S.vs, 2)
+        g.vector.tensor_tensor(T.sel[:, :], T.h2[:, 0:16], T.h2[:, 16:32], AluOpType.add).then_inc(S.sk, 1)
+
+        g.wait_ge(S.arr, n - 1)
+        fold = RemoteDMATransfer(dst_ids=[dst_id(r) for r in others], dma_engine_mask=wire, remote_sem=S.got,
+                                 srcs=[T.land[k] for k in range(n - 1)] + [T.stage[my]],
+                                 dsts=[T.res[my] for r in others], alu_op=1)
+        g.remote_dma_fused([fold], local_sem=S.loc)
+        left += ne
+
+        g.sync.wait_ge(S.arr, n - 1)
+        g.sync.dma_start(T.gath[:, :], T.land[:, :, :]).then_inc(S.gs, 16)
+        g.tensor.wait_ge(S.sk, 1)
+        g.tensor.wait_ge(S.gs, 16)
+        g.tensor.matmul(T.own[0:RW, 0:P], T.sel[:, :], T.gath[:, :], start=True, stop=True).then_inc(S.om, 1)
+        g.vector.wait_ge(S.ms, 16)
+        g.vector.wait_ge(S.om, 1)
+        g.vector.tensor_tensor(T.tot[0:RW, :], T.own[0:RW, 0:P], T.mine[0:RW, :], AluOpType.add).then_inc(S.ts, 1)
+        g.scalar.wait_ge(S.ts, 1)
+        g.scalar.dma_start(T.y[lo:hi, :], T.tot[0:RW, :]).then_inc(S.st2, 16)
+
+    stores = 0
+    if my is None:
+        g.sync.wait_ge(S.got, ne * NS)
+        g.sync.dma_start(T.y[:, :], T.res[:, :, :]).then_inc(S.st, 16)
+        stores = 1
+    else:
+        g.sync.wait_ge(S.got, ne * (NS - 1))
+        if my > 0:
+            g.sync.dma_start(T.y[0:RW * my, :], T.res[0:my]).then_inc(S.st, 16)
+            stores += 1
+        if my < NS - 1:
+            g.sync.dma_start(T.y[RW * (my + 1):P, :], T.res[my + 1:NS]).then_inc(S.st, 16)
+            stores += 1
+        g.scalar.wait_ge(S.st2, 16)
+    g.sync.wait_ge(S.st, 16 * stores)
+    g.wait_ge(S.loc, left)

@@ -4,6 +4,9 @@ from concourse.mybir import AluOpType
 P = 128
 NS = 8
 RW = P // NS
+DW = 16
+CW = P - DW
+SW = RW * CW // P
 
 SCRATCH = {
     "sah": ("sbuf", [P, P], "bfloat16"),
@@ -13,21 +16,21 @@ SCRATCH = {
     "acc": ("psum", [P, 512], "float32"),
     "own": ("psum", [P, 512], "float32"),
     "part": ("sbuf", [P, P], "float32"),
-    "stage": ("dram", [NS, P, RW], "float32"),
-    "land": ("dram", [NS, P, RW], "float32"),
-    "res": ("dram", [NS, P, RW], "float32"),
-    "seed": ("sbuf", [P, P + 1], "float32"),
-    "diag": ("dram", [P + 1, P], "float32"),
-    "eye": ("sbuf", [P, P], "float32"),
-    "h1": ("sbuf", [P, 64], "float32"),
-    "h2": ("sbuf", [P, 32], "float32"),
+    "stage": ("dram", [NS, P, SW], "float32"),
+    "land": ("dram", [NS, P, SW], "float32"),
+    "res": ("dram", [NS, P, SW], "float32"),
+    "landd": ("dram", [NS + 1, P, DW], "float32"),
+    "resd": ("dram", [P, DW], "float32"),
+    "seed": ("sbuf", [P, RW + 1], "float32"),
+    "shear": ("dram", [NS, RW * (RW + 1)], "float32"),
+    "seld": ("dram", [P, RW], "float32"),
     "sel": ("sbuf", [P, RW], "float32"),
-    "gath": ("sbuf", [P, P], "float32"),
-    "mine": ("sbuf", [P, P], "float32"),
-    "tot": ("sbuf", [P, P], "float32"),
+    "gath": ("sbuf", [P, CW], "float32"),
+    "mine": ("sbuf", [P, CW], "float32"),
+    "tot": ("sbuf", [P, CW], "float32"),
 }
 SEMAPHORES = ["ldh", "ldl", "mm", "cp", "staged", "arr", "got", "loc", "st", "st2",
-              "zs", "w1", "w2", "vs", "sk", "gs", "om", "ms", "ts"]
+              "zs", "w1", "w2", "sarr", "sk", "gs", "om", "ms", "ts", "arrd", "gotd"]
 
 
 def _bits(m):
@@ -35,29 +38,61 @@ def _bits(m):
 
 
 def rank_program(g, core, T, topo):
-    rank = T.rank_of(core)
-    if rank is None:
-        return
     S = T.sem
     cores = list(T.cores)
     n = len(cores)
-    others = [r for r in range(n) if r != rank]
-    for r in others:
-        if not topo.may_write(core, cores[r]):
-            raise ValueError("this plan needs every rank core to reach every other one by a write of its own")
+    rank = T.rank_of(core)
 
     peers = [sum(1 for b in cores if topo.same_plane(topo.chip(a), topo.chip(b))) for a in cores]
     idle = max(r for r in range(n) if peers[r] == max(peers))
     owners = [r for r in range(n) if r != idle]
-    my = owners.index(rank) if rank != idle else None
+    home = cores[idle]
+    spare = [c for c in range(topo.CHIPS * topo.CORES_PER_CHIP)
+             if topo.chip(c) == topo.chip(home) and topo.die(c) == topo.die(home) and c not in cores
+             and all(topo.may_write(c, d) for d in cores)]
+    helper = spare[0]
 
-    def dst_id(r):
-        rid, pid, _ = topo.addr(cores[r])
+    def dst_id(c):
+        rid, pid, _ = topo.addr(c)
         return DstId(rid=rid, pnc=pid)
 
-    wire = topo.mask(core, cores[others[0]])
+    def common_mask(dsts):
+        m = topo.mask(core, dsts[0])
+        for d in dsts:
+            m &= topo.mask(core, d)
+        return m
+
+    if core == helper:
+        wire = common_mask(cores)
+        ne = len(_bits(wire))
+        g.vector.memset(T.seed[:, 0:1], 1.0).then_inc(S.zs, 1)
+        g.vector.memset(T.seed[:, 1:RW + 1], 0.0).then_inc(S.zs, 1)
+        g.sync.wait_ge(S.zs, 2)
+        g.sync.dma_start(T.shear[:, :], T.seed[:, :]).then_inc(S.w1, 16)
+        g.sync.wait_ge(S.w1, 16)
+        g.scalar.wait_ge(S.w1, 16)
+        for j in range(NS):
+            q = g.sync if j % 2 == 0 else g.scalar
+            q.dma_start(T.seld[RW * j:RW * (j + 1), :], T.shear[j, 0:RW * RW]).then_inc(S.w2, 16)
+        g.wait_ge(S.w2, 16 * NS)
+        give = RemoteDMATransfer(dst_ids=[dst_id(cores[o]) for o in owners], dma_engine_mask=wire, remote_sem=S.sarr,
+                                 srcs=[T.seld[:, :]], dsts=[T.seld[:, :] for o in owners])
+        g.remote_dma_fused([give], local_sem=S.loc)
+        g.wait_ge(S.arrd, ne * n)
+        fold = RemoteDMATransfer(dst_ids=[dst_id(c) for c in cores], dma_engine_mask=wire, remote_sem=S.gotd,
+                                 srcs=[T.landd[k] for k in range(n)], dsts=[T.resd[:, :] for c in cores], alu_op=1)
+        g.remote_dma_fused([fold], local_sem=S.loc)
+        g.wait_ge(S.loc, 2 * ne)
+        return
+    if rank is None:
+        return
+
+    others = [r for r in range(n) if r != rank]
     for r in others:
-        wire &= topo.mask(core, cores[r])
+        if not topo.may_write(core, cores[r]):
+            raise ValueError("this plan needs every rank core to reach every other one by a write of its own")
+    my = owners.index(rank) if rank != idle else None
+    wire = common_mask([cores[r] for r in others] + [helper])
     eng = _bits(wire)
     ne = len(eng)
 
@@ -74,16 +109,15 @@ def rank_program(g, core, T, topo):
     g.tensor.matmul(acc, T.sal[:, :], T.sbh[:, :], start=False, stop=False)
     g.tensor.matmul(acc, T.sal[:, :], T.sbl[:, :], start=False, stop=True).then_inc(S.mm, 1)
 
-    if my is not None:
-        g.vector.memset(T.seed[:, 0:1], 1.0).then_inc(S.zs, 1)
-        g.vector.memset(T.seed[:, 1:P + 1], 0.0).then_inc(S.zs, 1)
-        g.scalar.wait_ge(S.zs, 2)
-        g.scalar.dma_start(T.diag[:, :], T.seed[:, :]).then_inc(S.w1, 16)
-
     g.vector.wait_ge(S.mm, 1)
     g.vector.tensor_copy(T.part[:, :], acc).then_inc(S.cp, 1)
     g.sync.wait_ge(S.cp, 1)
-    g.sync.dma_start(T.stage[:, :, :], T.part[:, :]).then_inc(S.staged, 16)
+    g.sync.dma_start(T.stage[:, :, :], T.part[:, DW:P]).then_inc(S.staged, 16)
+    g.wait_ge(S.cp, 1)
+    ahead = RemoteDMATransfer(dst_ids=[dst_id(helper)], dma_engine_mask=wire, remote_sem=S.arrd,
+                              src=T.part[:, 0:DW], dst=T.landd[rank])
+    g.remote_dma_fused([ahead], local_sem=S.loc)
+    left = ne
 
     g.wait_ge(S.staged, 16)
     sends = []
@@ -91,27 +125,20 @@ def rank_program(g, core, T, topo):
         if o == rank:
             continue
         slot = rank if rank < o else rank - 1
-        sends.append(RemoteDMATransfer(dst_ids=[dst_id(o)], dma_engine_mask=1 << eng[s % ne], remote_sem=S.arr,
+        sends.append(RemoteDMATransfer(dst_ids=[dst_id(cores[o])], dma_engine_mask=1 << eng[s % ne], remote_sem=S.arr,
                                        src=T.stage[s], dst=T.land[slot]))
     g.remote_dma_fused(sends, local_sem=S.loc)
-    left = len(sends)
+    left += len(sends)
 
     if my is not None:
         lo, hi = RW * my, RW * (my + 1)
-        g.scalar.wait_ge(S.w1, 16)
-        g.scalar.wait_ge(S.staged, 16)
-        g.scalar.dma_start(T.eye[:, :], T.diag[0:P, :]).then_inc(S.w2, 16)
         g.scalar.wait_ge(S.cp, 1)
-        g.scalar.dma_start(T.mine[0:RW, :], T.part[lo:hi, :]).then_inc(S.ms, 16)
-        g.vector.wait_ge(S.w2, 16)
-        g.vector.tensor_tensor(T.h1[:, :], T.eye[:, 0:64], T.eye[:, 64:128], AluOpType.add).then_inc(S.vs, 1)
-        g.vector.wait_ge(S.vs, 1)
-        g.vector.tensor_tensor(T.h2[:, :], T.h1[:, 0:32], T.h1[:, 32:64], AluOpType.add).then_inc(S.vs, 1)
-        g.vector.wait_ge(S.vs, 2)
-        g.vector.tensor_tensor(T.sel[:, :], T.h2[:, 0:16], T.h2[:, 16:32], AluOpType.add).then_inc(S.sk, 1)
+        g.scalar.dma_start(T.mine[0:RW, :], T.part[lo:hi, DW:P]).then_inc(S.ms, 16)
+        g.scalar.wait_ge(S.sarr, ne)
+        g.scalar.dma_start(T.sel[:, :], T.seld[:, :]).then_inc(S.sk, 16)
 
         g.wait_ge(S.arr, n - 1)
-        fold = RemoteDMATransfer(dst_ids=[dst_id(r) for r in others], dma_engine_mask=wire, remote_sem=S.got,
+        fold = RemoteDMATransfer(dst_ids=[dst_id(cores[r]) for r in others], dma_engine_mask=wire, remote_sem=S.got,
                                  srcs=[T.land[k] for k in range(n - 1)] + [T.stage[my]],
                                  dsts=[T.res[my] for r in others], alu_op=1)
         g.remote_dma_fused([fold], local_sem=S.loc)
@@ -119,28 +146,32 @@ def rank_program(g, core, T, topo):
 
         g.sync.wait_ge(S.arr, n - 1)
         g.sync.dma_start(T.gath[:, :], T.land[:, :, :]).then_inc(S.gs, 16)
-        g.tensor.wait_ge(S.sk, 1)
+        g.tensor.wait_ge(S.sk, 16)
         g.tensor.wait_ge(S.gs, 16)
-        g.tensor.matmul(T.own[0:RW, 0:P], T.sel[:, :], T.gath[:, :], start=True, stop=True).then_inc(S.om, 1)
+        g.tensor.matmul(T.own[0:RW, 0:CW], T.sel[:, :], T.gath[:, :], start=True, stop=True).then_inc(S.om, 1)
         g.vector.wait_ge(S.ms, 16)
         g.vector.wait_ge(S.om, 1)
-        g.vector.tensor_tensor(T.tot[0:RW, :], T.own[0:RW, 0:P], T.mine[0:RW, :], AluOpType.add).then_inc(S.ts, 1)
-        g.scalar.wait_ge(S.ts, 1)
-        g.scalar.dma_start(T.y[lo:hi, :], T.tot[0:RW, :]).then_inc(S.st2, 16)
+        g.vector.tensor_tensor(T.tot[0:RW, :], T.own[0:RW, 0:CW], T.mine[0:RW, :], AluOpType.add).then_inc(S.ts, 1)
 
+    g.scalar.wait_ge(S.gotd, ne)
+    g.scalar.dma_start(T.y[:, 0:DW], T.resd[:, :]).then_inc(S.st2, 16)
+    late = 1
     stores = 0
     if my is None:
         g.sync.wait_ge(S.got, ne * NS)
-        g.sync.dma_start(T.y[:, :], T.res[:, :, :]).then_inc(S.st, 16)
+        g.sync.dma_start(T.y[:, DW:P], T.res[:, :, :]).then_inc(S.st, 16)
         stores = 1
     else:
+        g.scalar.wait_ge(S.ts, 1)
+        g.scalar.dma_start(T.y[lo:hi, DW:P], T.tot[0:RW, :]).then_inc(S.st2, 16)
+        late += 1
         g.sync.wait_ge(S.got, ne * (NS - 1))
         if my > 0:
-            g.sync.dma_start(T.y[0:RW * my, :], T.res[0:my]).then_inc(S.st, 16)
+            g.sync.dma_start(T.y[0:lo, DW:P], T.res[0:my]).then_inc(S.st, 16)
             stores += 1
         if my < NS - 1:
-            g.sync.dma_start(T.y[RW * (my + 1):P, :], T.res[my + 1:NS]).then_inc(S.st, 16)
+            g.sync.dma_start(T.y[hi:P, DW:P], T.res[my + 1:NS]).then_inc(S.st, 16)
             stores += 1
-        g.scalar.wait_ge(S.st2, 16)
+    g.scalar.wait_ge(S.st2, 16 * late)
     g.sync.wait_ge(S.st, 16 * stores)
     g.wait_ge(S.loc, left)

from concourse.bass import DstId, RemoteDMATransfer
from concourse.mybir import AluOpType

P = 128
NS = 8
RW = P // NS
DW = 16
CW = P - DW
SW = RW * CW // P

SCRATCH = {
    "sah": ("sbuf", [P, P], "bfloat16"),
    "sal": ("sbuf", [P, P], "bfloat16"),
    "sbh": ("sbuf", [P, P], "bfloat16"),
    "sbl": ("sbuf", [P, P], "bfloat16"),
    "acc": ("psum", [P, 512], "float32"),
    "own": ("psum", [P, 512], "float32"),
    "part": ("sbuf", [P, P], "float32"),
    "stage": ("dram", [NS, P, SW], "float32"),
    "land": ("dram", [NS, P, SW], "float32"),
    "res": ("dram", [NS, P, SW], "float32"),
    "landd": ("dram", [NS + 1, P, DW], "float32"),
    "resd": ("dram", [P, DW], "float32"),
    "seed": ("sbuf", [P, RW + 1], "float32"),
    "shear": ("dram", [NS, RW * (RW + 1)], "float32"),
    "seld": ("dram", [P, RW], "float32"),
    "sel": ("sbuf", [P, RW], "float32"),
    "gath": ("sbuf", [P, CW], "float32"),
    "mine": ("sbuf", [P, CW], "float32"),
    "tot": ("sbuf", [P, CW], "float32"),
}
SEMAPHORES = ["ldh", "ldl", "mm", "cp", "staged", "arr", "got", "loc", "st", "st2",
              "zs", "w1", "w2", "sarr", "sk", "gs", "om", "ms", "ts", "arrd", "gotd"]


def _bits(m):
    return [b for b in range(m.bit_length()) if (m >> b) & 1]


def rank_program(g, core, T, topo):
    S = T.sem
    cores = list(T.cores)
    n = len(cores)
    rank = T.rank_of(core)

    peers = [sum(1 for b in cores if topo.same_plane(topo.chip(a), topo.chip(b))) for a in cores]
    idle = max(r for r in range(n) if peers[r] == max(peers))
    owners = [r for r in range(n) if r != idle]
    home = cores[idle]
    spare = [c for c in range(topo.CHIPS * topo.CORES_PER_CHIP)
             if topo.chip(c) == topo.chip(home) and topo.die(c) == topo.die(home) and c not in cores
             and all(topo.may_write(c, d) for d in cores)]
    helper = spare[0]

    def dst_id(c):
        rid, pid, _ = topo.addr(c)
        return DstId(rid=rid, pnc=pid)

    def common_mask(dsts):
        m = topo.mask(core, dsts[0])
        for d in dsts:
            m &= topo.mask(core, d)
        return m

    if core == helper:
        wire = common_mask(cores)
        ne = len(_bits(wire))
        g.vector.memset(T.seed[:, 0:1], 1.0).then_inc(S.zs, 1)
        g.vector.memset(T.seed[:, 1:RW + 1], 0.0).then_inc(S.zs, 1)
        g.sync.wait_ge(S.zs, 2)
        g.sync.dma_start(T.shear[:, :], T.seed[:, :]).then_inc(S.w1, 16)
        g.sync.wait_ge(S.w1, 16)
        g.scalar.wait_ge(S.w1, 16)
        for j in range(NS):
            q = g.sync if j % 2 == 0 else g.scalar
            q.dma_start(T.seld[RW * j:RW * (j + 1), :], T.shear[j, 0:RW * RW]).then_inc(S.w2, 16)
        g.wait_ge(S.w2, 16 * NS)
        give = RemoteDMATransfer(dst_ids=[dst_id(cores[o]) for o in owners], dma_engine_mask=wire, remote_sem=S.sarr,
                                 srcs=[T.seld[:, :]], dsts=[T.seld[:, :] for o in owners])
        g.remote_dma_fused([give], local_sem=S.loc)
        g.wait_ge(S.arrd, ne * n)
        fold = RemoteDMATransfer(dst_ids=[dst_id(c) for c in cores], dma_engine_mask=wire, remote_sem=S.gotd,
                                 srcs=[T.landd[k] for k in range(n)], dsts=[T.resd[:, :] for c in cores], alu_op=1)
        g.remote_dma_fused([fold], local_sem=S.loc)
        g.wait_ge(S.loc, 2 * ne)
        return
    if rank is None:
        return

    others = [r for r in range(n) if r != rank]
    for r in others:
        if not topo.may_write(core, cores[r]):
            raise ValueError("this plan needs every rank core to reach every other one by a write of its own")
    my = owners.index(rank) if rank != idle else None
    wire = common_mask([cores[r] for r in others] + [helper])
    eng = _bits(wire)
    ne = len(eng)

    g.sync.dma_start(T.sah[:, :], T.ah[:, :]).then_inc(S.ldh, 16)
    g.scalar.dma_start(T.sbh[:, :], T.bh[:, :]).then_inc(S.ldh, 16)
    g.sync.dma_start(T.sal[:, :], T.al[:, :]).then_inc(S.ldl, 16)
    g.scalar.dma_start(T.sbl[:, :], T.bl[:, :]).then_inc(S.ldl, 16)

    acc = T.acc[:, 0:P]
    g.tensor.wait_ge(S.ldh, 32)
    g.tensor.matmul(acc, T.sah[:, :], T.sbh[:, :], start=True, stop=False)
    g.tensor.wait_ge(S.ldl, 32)
    g.tensor.matmul(acc, T.sah[:, :], T.sbl[:, :], start=False, stop=False)
    g.tensor.matmul(acc, T.sal[:, :], T.sbh[:, :], start=False, stop=False)
    g.tensor.matmul(acc, T.sal[:, :], T.sbl[:, :], start=False, stop=True).then_inc(S.mm, 1)

    g.vector.wait_ge(S.mm, 1)
    g.vector.tensor_copy(T.part[:, :], acc).then_inc(S.cp, 1)
    g.sync.wait_ge(S.cp, 1)
    g.sync.dma_start(T.stage[:, :, :], T.part[:, DW:P]).then_inc(S.staged, 16)
    g.wait_ge(S.cp, 1)
    ahead = RemoteDMATransfer(dst_ids=[dst_id(helper)], dma_engine_mask=wire, remote_sem=S.arrd,
                              src=T.part[:, 0:DW], dst=T.landd[rank])
    g.remote_dma_fused([ahead], local_sem=S.loc)
    left = ne

    g.wait_ge(S.staged, 16)
    sends = []
    for s, o in enumerate(owners):
        if o == rank:
            continue
        slot = rank if rank < o else rank - 1
        sends.append(RemoteDMATransfer(dst_ids=[dst_id(cores[o])], dma_engine_mask=1 << eng[s % ne], remote_sem=S.arr,
                                       src=T.stage[s], dst=T.land[slot]))
    g.remote_dma_fused(sends, local_sem=S.loc)
    left += len(sends)

    if my is not None:
        lo, hi = RW * my, RW * (my + 1)
        g.scalar.wait_ge(S.cp, 1)
        g.scalar.dma_start(T.mine[0:RW, :], T.part[lo:hi, DW:P]).then_inc(S.ms, 16)
        g.scalar.wait_ge(S.sarr, ne)
        g.scalar.dma_start(T.sel[:, :], T.seld[:, :]).then_inc(S.sk, 16)

        g.wait_ge(S.arr, n - 1)
        fold = RemoteDMATransfer(dst_ids=[dst_id(cores[r]) for r in others], dma_engine_mask=wire, remote_sem=S.got,
                                 srcs=[T.land[k] for k in range(n - 1)] + [T.stage[my]],
                                 dsts=[T.res[my] for r in others], alu_op=1)
        g.remote_dma_fused([fold], local_sem=S.loc)
        left += ne

        g.sync.wait_ge(S.arr, n - 1)
        g.sync.dma_start(T.gath[:, :], T.land[:, :, :]).then_inc(S.gs, 16)
        g.tensor.wait_ge(S.sk, 16)
        g.tensor.wait_ge(S.gs, 16)
        g.tensor.matmul(T.own[0:RW, 0:CW], T.sel[:, :], T.gath[:, :], start=True, stop=True).then_inc(S.om, 1)
        g.vector.wait_ge(S.ms, 16)
        g.vector.wait_ge(S.om, 1)
        g.vector.tensor_tensor(T.tot[0:RW, :], T.own[0:RW, 0:CW], T.mine[0:RW, :], AluOpType.add).then_inc(S.ts, 1)

    g.scalar.wait_ge(S.gotd, ne)
    g.scalar.dma_start(T.y[:, 0:DW], T.resd[:, :]).then_inc(S.st2, 16)
    late = 1
    stores = 0
    if my is None:
        g.sync.wait_ge(S.got, ne * NS)
        g.sync.dma_start(T.y[:, DW:P], T.res[:, :, :]).then_inc(S.st, 16)
        stores = 1
    else:
        g.scalar.wait_ge(S.ts, 1)
        g.scalar.dma_start(T.y[lo:hi, DW:P], T.tot[0:RW, :]).then_inc(S.st2, 16)
        late += 1
        g.sync.wait_ge(S.got, ne * (NS - 1))
        if my > 0:
            g.sync.dma_start(T.y[0:lo, DW:P], T.res[0:my]).then_inc(S.st, 16)
            stores += 1
        if my < NS - 1:
            g.sync.dma_start(T.y[hi:P, DW:P], T.res[my + 1:NS]).then_inc(S.st, 16)
            stores += 1
    g.scalar.wait_ge(S.st2, 16 * late)
    g.sync.wait_ge(S.st, 16 * stores)
    g.wait_ge(S.loc, left)
